import numpy as np, ml_dtypes
CORES = [23,39,55,63,87,103,111,127,18,34,50,58,82,98,106,122]
N = 16
NB, B = 3, 512
def setup_inputs(rng):
    return {"x": rng.standard_normal((N, 128, NB * B), dtype=np.float32).astype(ml_dtypes.bfloat16), "wv": (rng.standard_normal((N, 128, 128), dtype=np.float32) / 16).astype(ml_dtypes.bfloat16), "wh": (rng.standard_normal((N, 128, 128), dtype=np.float32) / 16).astype(ml_dtypes.bfloat16)}
def setup_inputs_big(rng):
    d = setup_inputs(rng)
    for k in ("x",): d[k] = (d[k].astype(np.float32) * 1048576.0).astype(d[k].dtype)
    return d
def setup_inputs_small(rng):
    d = setup_inputs(rng)
    for k in ("x",): d[k] = (d[k].astype(np.float32) * (1 / 1048576.0)).astype(d[k].dtype)
    return d
def setup_inputs_apart(rng):
    d = setup_inputs(rng)
    f = (10.0 ** rng.permutation(np.linspace(-1.5, 1.5, N))).astype(np.float32).reshape(N, 1, 1)
    for k in ("x",): d[k] = (d[k].astype(np.float32) * f).astype(d[k].dtype)
    return d
def reference(x, wv, wh):
    X, WV, WH = x.astype(np.float64), wv.astype(np.float64), wh.astype(np.float64)
    h = np.zeros((N, NB, 128, B))
    for r in range(N):
        for c in range(NB):
            a = X[r][:, B * c:B * c + B].copy()
            if r: a += WV[r].T @ h[r - 1][c]
            if c: a += WH[r].T @ h[r][c - 1]
            h[r][c] = np.maximum(a, 0.0)
    return {"y": np.concatenate([h[:, c] for c in range(NB)], axis=2).astype(ml_dtypes.bfloat16)}

from concourse.bass import DstId, RemoteDMATransfer
from concourse.mybir import AluOpType

SIZES = (4, 4, 8)
NSEP = 1
LOOK = 4
NB, B = 3, 512
NBANK = 8
WC = 256

SCRATCH = {
    "xsb": ("sbuf", [128, NB * B], "bfloat16"),
    "wsb": ("sbuf", [128, WC], "bfloat16"),
    "ida": ("sbuf", [128, 129], "bfloat16"),
    "idd": ("dram", [129, 128], "bfloat16"),
    "ident": ("sbuf", [128, 128], "bfloat16"),
    "zeros": ("sbuf", [128, B], "float32"),
}
for _k in range(NBANK):
    SCRATCH["ps%d" % _k] = ("psum", [128, 512], "float32")
for _g in sorted(set(SIZES)):
    _w = B // _g
    SCRATCH["yl%d" % _g] = ("sbuf", [128, _g, NB, _w], "bfloat16")
    SCRATCH["hin%d" % _g] = ("sbuf", [128, NB, _w], "bfloat16")
    if _g > 1:
        SCRATCH["stage%d" % _g] = ("sbuf", [128, _g, WC + NB * _w], "bfloat16")
        SCRATCH["land%d" % _g] = ("sbuf", [128, _g, WC + NB * _w], "bfloat16")
        SCRATCH["hbuf%d" % _g] = ("sbuf", [128, _g, NB, _w], "bfloat16")
        SCRATCH["ysb%d" % _g] = ("sbuf", [128, NB, _g, _w], "bfloat16")

SEMAPHORES = (["ld_w", "ld_x", "idm", "id1", "id2", "zs", "stg", "lsem", "mm", "vv", "yarr", "pm", "sta", "stb"]
              + ["arr%d" % _k for _k in range(max(SIZES))] + ["hin%d" % _k for _k in range(NB)])


def _plan(T, topo):
    st, r0 = [], 0
    for gs in SIZES:
        st.append((r0, gs))
        r0 += gs

    def dist(a, b):
        ca, cb = topo.chip(a), topo.chip(b)
        if ca == cb:
            return 0
        return 1 if (topo.same_plane(ca, cb) or topo.mates(ca, cb)) else 2

    maps = []
    for i, (r0, gs) in enumerate(st):
        if i == 0:
            maps.append(list(range(gs)))
            continue
        p0, pg = st[i - 1]
        m = gs // pg
        mp, free = [None] * gs, list(range(gs))
        for level in (0, 1, 2):
            for sh in range(gs):
                if mp[sh] is None:
                    src = T.cores[p0 + maps[i - 1][sh // m]]
                    for rr in free:
                        if dist(src, T.cores[r0 + rr]) == level:
                            mp[sh] = rr
                            free.remove(rr)
                            break
        maps.append(mp)
    return st, maps


def rank_program(g, core, T, topo):
    R = T.rank_of(core)
    if R is None:
        return
    st, maps = _plan(T, topo)

    def stage_of(rk):
        for i, (a, n) in enumerate(st):
            if a <= rk < a + n:
                return i

    def hop_dests(rk):
        i = stage_of(rk)
        if i + 1 == len(st):
            return []
        a, n = st[i]
        a2, n2 = st[i + 1]
        m = n2 // n
        sh = maps[i].index(rk - a)
        return [a2 + maps[i + 1][sh * m + t] for t in range(m)]

    def engines(rk):
        a, n = st[stage_of(rk)]
        mk = None
        for d in [a + k for k in range(n) if a + k != rk] + hop_dests(rk):
            assert topo.may_write(T.cores[rk], T.cores[d])
            e = topo.mask(T.cores[rk], T.cores[d])
            mk = e if mk is None else mk & e
        return [1 << b for b in range(mk.bit_length()) if (mk >> b) & 1]

    si = stage_of(R)
    r0, gs = st[si]
    me = R - r0
    shard = maps[si].index
    sh = shard(me)
    W = B // gs
    eng = engines(R)
    ne, full = len(eng), sum(eng)
    S = T.sem
    yl, hin = T["yl%d" % gs], T["hin%d" % gs]
    if gs > 1:
        stage, land, hbuf, ysb = T["stage%d" % gs], T["land%d" % gs], T["hbuf%d" % gs], T["ysb%d" % gs]
    ps = [T["ps%d" % k] for k in range(NBANK)]
    te, v, sy, sc = g.tensor, g.vector, g.sync, g.scalar
    woff = 128 if R == 0 else 0
    nld = 16 if R == 0 else 32

    seen = {}

    def wait(q, qn, name, val):
        if seen.get((qn, name), 0) < val:
            seen[(qn, name)] = val
            q.wait_ge(S[name], val)

    sent = [0]

    def send(rk, out_ap, in_ap, rsem):
        rid, pid, _ = topo.addr(T.cores[rk])
        g.remote_dma(out_ap=out_ap, in_ap=in_ap, remote_sem=rsem, local_sem=S.lsem, pid=pid, routing_id=rid,
                     dma_engine_mask=full)
        sent[0] += ne

    if R > 0:
        sy.dma_start(T.wsb[:, 0:128], T.wv[:]).then_inc(S.ld_w, 16)
    sy.dma_start(T.wsb[:, 128:256], T.wh[:]).then_inc(S.ld_w, 16)
    sc.dma_start(T.xsb[:], T.x[:]).then_inc(S.ld_x, 16)
    v.memset(T.ida[:, 1:129], 0.0).then_inc(S.idm, 1)
    v.memset(T.ida[:, 0:1], 1.0).then_inc(S.idm, 1)
    v.memset(T.zeros[:, 0:W], 0.0).then_inc(S.zs, 1)
    wait(sy, "sy", "idm", 2)
    sy.dma_start(T.idd[:], T.ida[:]).then_inc(S.id1, 16)
    wait(sy, "sy", "id1", 16)
    sy.dma_start(T.ident[:], T.idd[0:128, :]).then_inc(S.id2, 16)

    ds = [(me + k) % gs for k in range(1, gs)]
    sep = ds[:NSEP]
    if gs > 1:
        wait(g, "g", "ld_w", nld)
        for d in sep:
            send(r0 + d, land[:, me, woff:WC], T.wsb[:, woff:WC], S["arr%d" % me])
        wait(v, "v", "ld_w", nld)
        nw = 0
        for d in ds[NSEP:]:
            v.tensor_copy(stage[:, d, woff:WC], T.wsb[:, woff:WC]).then_inc(S.stg, 1)
            nw += 1
        wait(v, "v", "ld_x", 16)
        for k, d in enumerate(ds):
            for c in range(NB):
                lo = c * B + shard(d) * W
                v.tensor_copy(stage[:, d, WC + c * W:WC + (c + 1) * W], T.xsb[:, lo:lo + W]).then_inc(S.stg, 1)
            wait(g, "g", "stg", nw + NB * (k + 1))
            lo = WC if d in sep else woff
            send(r0 + d, land[:, me, lo:], stage[:, d, lo:], S["arr%d" % me])

    cells = sorted(((rr, c) for rr in range(gs) for c in range(NB)), key=lambda t: (t[0] + t[1], t[1]))
    idx = {cell: k for k, cell in enumerate(cells)}
    n = len(cells)

    def hloc(rr, c, lo=0, hi=None):
        hi = W if hi is None else hi
        return yl[:, sh, c, lo:hi] if rr == me else hbuf[:, rr, c, lo:hi]

    def xloc(rr, c):
        if rr == me:
            return T.xsb[:, c * B + sh * W:c * B + (sh + 1) * W]
        return land[:, rr, WC + c * W:WC + (c + 1) * W]

    def wloc(rr, k):
        return T.wsb[:, 128 * k:128 * k + 128] if rr == me else land[:, rr, 128 * k:128 * k + 128]

    def preload(j):
        rr, c = cells[j]
        if rr == me:
            wait(te, "te", "ld_w", nld)
            wait(te, "te", "ld_x", 16)
        else:
            writes = 2 if 1 <= (me - rr) % gs <= NSEP else 1
            wait(te, "te", "arr%d" % rr, writes * len(engines(r0 + rr)))
        wait(te, "te", "id2", 16)
        if j >= NBANK:
            wait(te, "te", "vv", j - NBANK + 1)
        only = (r0 + rr == 0 and c == 0)
        ins = te.matmul(ps[j % NBANK][:, 0:W], T.ident[:], xloc(rr, c), True, only)
        if only:
            ins.then_inc(S.mm, 1)

    if si > 0:
        p0, pg = st[si - 1]
        feeder = p0 + maps[si - 1][sh // (gs // pg)]
        hin_n = len(engines(feeder)) // (gs // pg)

    for j in range(min(LOOK, n)):
        preload(j)
    wait(v, "v", "zs", 1)
    for k, (rr, c) in enumerate(cells):
        if k + LOOK < n:
            preload(k + LOOK)
        ops = []
        if c > 0:
            ops.append((wloc(rr, 1), hloc(rr, c - 1), "vv", idx[(rr, c - 1)] + 1))
        if rr > 0:
            ops.append((wloc(rr, 0), hloc(rr - 1, c), "vv", idx[(rr - 1, c)] + 1))
        elif r0 > 0:
            ops.append((wloc(rr, 0), hin[:, c, :], "hin%d" % c, hin_n))
        for t, (w, h, name, val) in enumerate(ops):
            wait(te, "te", name, val)
            ins = te.matmul(ps[k % NBANK][:, 0:W], w, h, False, t == len(ops) - 1)
            if t == len(ops) - 1:
                ins.then_inc(S.mm, 1)
        wait(v, "v", "mm", k + 1)
        v.tensor_tensor(hloc(rr, c), ps[k % NBANK][:, 0:W], T.zeros[:, 0:W], AluOpType.max).then_inc(S.vv, 1)

    nxt = hop_dests(R)
    if nxt:
        m = len(nxt)
        g2 = st[si + 1][1]
        W2 = B // g2
        per = ne // m
        for c in range(NB):
            wait(g, "g", "vv", idx[(gs - 1, c)] + 1)
            if m == 1:
                send(nxt[0], T["hin%d" % g2][:, c, :], hloc(gs - 1, c), S["hin%d" % c])
            else:
                trs = []
                for t, d in enumerate(nxt):
                    rid, pid, _ = topo.addr(T.cores[d])
                    trs.append(RemoteDMATransfer(dst_ids=[DstId(rid=rid, pnc=pid)],
                                                 dma_engine_mask=sum(eng[t * per:(t + 1) * per]),
                                                 remote_sem=S["hin%d" % c],
                                                 src=hloc(gs - 1, c, t * W2, (t + 1) * W2),
                                                 dst=T["hin%d" % g2][:, c, :]))
                g.remote_dma_fused(trs, local_sem=S.lsem)
                sent[0] += per * m

    for rr in range(gs):
        if rr != me:
            wait(g, "g", "vv", idx[(rr, NB - 1)] + 1)
            send(r0 + rr, yl[:, sh, :, :], hbuf[:, rr, :, :], S.yarr)
    if sent[0]:
        wait(g, "g", "lsem", sent[0])

    if gs > 1:
        wait(v, "v", "vv", n)
        wait(v, "v", "yarr", sum(len(engines(r0 + k)) for k in range(gs) if k != me))
    nst = {"sy": 0, "sc": 0}
    for c in range(NB):
        q, qn, sem = (sy, "sy", S.sta) if c % 2 == 0 else (sc, "sc", S.stb)
        if gs > 1:
            v.tensor_copy(ysb[:, c, :, :], yl[:, :, c, :]).then_inc(S.pm, 1)
            wait(q, qn, "pm", c + 1)
            src = ysb[:, c, :, :]
        else:
            wait(q, qn, "vv", idx[(0, c)] + 1)
            src = yl[:, 0, c, :]
        q.dma_start(T.y[:, c * B:(c + 1) * B], src).then_inc(sem, 16)
        nst[qn] += 16
    wait(sy, "sy", "sta", nst["sy"])
    wait(sc, "sc", "stb", nst["sc"])
